import numpy as np
import ml_dtypes


def mxq(x, axis, fmt="e4m3"):
    dtype, down = {"e4m3": (ml_dtypes.float8_e4m3fn, 7), "e5m2": (ml_dtypes.float8_e5m2, 14)}[fmt]
    v = np.moveaxis(np.asarray(x, np.float32).astype(ml_dtypes.bfloat16).astype(np.float64), axis, -1)
    blocks = v.reshape(v.shape[:-1] + (-1, 32))
    amax = np.abs(blocks).max(-1, keepdims=True)
    byte = np.maximum(np.where(amax > 0, np.frexp(amax)[1] - 1 + 127, 0) - down, 1)
    scale = np.exp2(byte - 127.0)
    codes = (blocks / scale).astype(np.float32).astype(dtype).astype(np.float64)
    return np.moveaxis((codes * scale).reshape(v.shape), -1, axis)


WIDE = False


def mx_kscale(k):
    if not WIDE:
        return np.ones(k)
    levels = np.array([10, -10, 5, -5, 0])
    if k % 512:
        return np.exp2(np.random.permutation(np.resize(levels, k // 32))).repeat(32)
    a = np.empty((k // 512, 16))
    for p in range(k // 512):
        a[p, :8] = np.random.permutation(np.resize(levels, 8))
        for g in range(8):
            far = levels[np.abs(levels - a[p, g]) >= 10]
            a[p, g + 8] = far[np.random.randint(len(far))]
    return np.exp2(a.ravel()).repeat(32)


BF16 = ml_dtypes.bfloat16


def bf(x):
    return np.asarray(x, np.float32).astype(BF16)


def f64(x):
    return np.asarray(x).astype(np.float64)


E2M1 = np.array([0.0, 0.5, 1.0, 1.5, 2.0, 3.0, 4.0, 6.0, -0.0, -0.5, -1.0, -1.5, -2.0, -3.0, -4.0, -6.0])


def pack_weight(w, fmt):
    k, n = w.shape
    w = f64(bf(w)).reshape(k // 32, 32, n)
    amax = np.abs(w).max(1)
    if fmt == "e4m3":
        byte = np.frexp(amax)[1] - 1 + 127 - 7
    else:
        mant, ex = np.frexp(amax / 6.0)
        byte = np.where(mant > 0.5, ex, ex - 1) + 127
    byte = np.clip(np.where(amax > 0, byte, 1), 1, 254)
    scaled = (w * np.exp2(127.0 - byte)[:, None, :]).reshape(k, n).astype(np.float32)
    by_word = np.ascontiguousarray(scaled.reshape(k // 512, 128, 4, n).transpose(0, 1, 3, 2))
    if fmt == "e4m3":
        words = by_word.astype(ml_dtypes.float8_e4m3fn).view(np.uint8)
    else:
        c = by_word.astype(ml_dtypes.float4_e2m1fn).view(np.uint8) & 0xF
        words = c[..., 0::2] | (c[..., 1::2] << 4)
    return np.ascontiguousarray(words), np.ascontiguousarray(byte.astype(np.uint8).reshape(k // 512, 16, n))


def unpack_weight(words, scales, fmt):
    g, p, n, _ = words.shape
    if fmt == "e4m3":
        vals = np.ascontiguousarray(words).view(ml_dtypes.float8_e4m3fn).astype(np.float64)
    else:
        nib = np.empty((g, p, n, 4), np.uint8)
        nib[..., 0::2] = words & 0xF
        nib[..., 1::2] = words >> 4
        vals = E2M1[nib]
    vals = vals * np.repeat(np.exp2(scales.astype(np.float64) - 127.0), 8, axis=1)[..., None]
    return vals.transpose(0, 1, 3, 2).reshape(g * 512, n)
def pack4(w):
    words, scales = pack_weight(w, "e2m1")
    return words.reshape(words.shape[0], 128, -1), scales


def unpack4(words, scales):
    return unpack_weight(words.reshape(words.shape[0], 128, -1, 2), scales, "e2m1")


M, K, N, R, T = 3072, 1024, 1024, 512, 128


def draw0():
    s, t, u = mx_kscale(K), mx_kscale(N), mx_kscale(M)
    jl = np.random.standard_normal((N, R)) / np.sqrt(N) / t[:, None]
    jl_words, jl_scales = pack4(jl)
    return {"a": bf(np.random.standard_normal((M, K)) * s),
            "rinv": bf(np.random.standard_normal((K, N)) / np.sqrt(K) / s[:, None] * t),
            "w": bf(np.exp(0.3 * np.random.standard_normal(M)) * u),
            "jl_words": jl_words,
            "jl_scales": jl_scales,
            "b": bf(np.random.standard_normal((T, M)) / np.sqrt(M) / u)}


def core(a, rinv, w, jl_words, jl_scales, b):
    h = mxq(f64(a), 1, "e4m3") @ mxq(f64(rinv), 0, "e4m3")
    h = h * f64(w)[:, None]
    y = mxq(h, 1, "e4m3") @ unpack4(jl_words, jl_scales)
    lev = np.mean(np.square(y), axis=1)
    c = mxq(f64(b), 1, "e4m3") @ mxq(h, 0, "e4m3")
    return y, lev, c


def e4m3fn_bytes(y):
    return np.clip(np.asarray(y, np.float64), -448.0, 448.0).astype(np.float32).astype(ml_dtypes.float8_e4m3fn).view(np.uint8)


def e4m3fn_values(b):
    return np.asarray(b, np.uint8).view(ml_dtypes.float8_e4m3fn).astype(np.float64)


def setup_inputs():
    d = draw0()
    x0 = np.asarray(d['a']).astype(np.float64)
    s = (np.max(np.abs(x0), axis=(0,), keepdims=True) / 448.0).astype(np.float32)
    out = {}
    for k, v in d.items():
        if k == 'a':
            out['a_bytes'] = e4m3fn_bytes(x0 / s.astype(np.float64))
            out['a_scale'] = s
        else:
            out[k] = v
    return out


def reference(a_bytes, a_scale, rinv, w, jl_words, jl_scales, b):
    return core(e4m3fn_values(a_bytes) * a_scale.astype(np.float64), rinv, w, jl_words, jl_scales, b)

@@ -1,0 +1,401 @@
+from contextlib import ExitStack
+
+import concourse.mybir as mybir
+from concourse.masks import make_identity
+
+M, K, N, R, T = 3072, 1024, 1024, 512, 128
+FLOPS = 2 * M * K * N + 2 * M * N * R + 2 * T * M * N
+
+F32 = mybir.dt.float32
+BF16 = mybir.dt.bfloat16
+I32 = mybir.dt.int32
+U32 = mybir.dt.uint32
+U8 = mybir.dt.uint8
+FP8 = mybir.dt.float8_e4m3fn
+FP8X4 = mybir.dt.float8_e4m3fn_x4
+FP4X4 = mybir.dt.float4_e2m1fn_x4
+MULT = mybir.AluOpType.mult
+COPY = mybir.ActivationFunctionType.Copy
+SQUARE = mybir.ActivationFunctionType.Square
+
+P = 128
+X_DMA = ["a0", "r00", "r11", "r01", "r10", "a1", "a2", "j", "a4", "a3", "a7", "a6", "a5", "a8", "a9", "b", "a10", "a11"]
+X_SC = "vs"
+PTR, PH, PY = 2, 3, 3
+ORDER = [("TA", 0, 1), ("R", 0, 1), ("IC0", 2, 1), ("TH", 2, 1), ("EA", 0, 1), ("EY", 4, 1), ("H0", 1, 1), ("EH", 2, 1), ("H1", 1, 1), ("P", -2, 1), ("E0", 1, 1), ("QA", 0, 1), ("QC1", 4, 1), ("QC0", 3, 1), ("QH", 2, 1), ("E1", 1, 1), ("B", 0, 1), ("Y", 3, 1), ("LV", 5, 1), ("IC1", 3, 1)]
+RINV = [(1, "I", 0, 1, 0, "s"), (1, "Q", 0, 1), (-2, "I", 0, 0, 1, "s"), (1, "Q", 1, 1), (-2, "I", 1, 1, 0, "s"), (-1, "Q", 0, 0), (0, "I", 1, 0, 1, "s"), (-2, "I", 0, 0, 0, "v"), (0, "I", 1, 0, 0, "v"), (0, "Q", 1, 0), (-1, "I", 1, 1, 1, "v"), (-1, "I", 0, 1, 1, "v")]
+X_EA = ("sssv", 3, 26)
+X_EH = ("ssss", 1, 38)
+X_EY = ("vvss", 0, 18)
+X_EE = ("ssssssss", 5, 50)
+BSTART, BENG, CSTART, CENG = 16, "s", 31, "sv"
+GROUPS = M // 512
+TILES = M // P
+KG = K // 512
+NG = N // 512
+
+
+def tile_weighted_leverage_sketch_s8_kernel(
+    tc, a_bytes, a_scale, rinv, w, jl_words, jl_scales, b, y, lev, c
+):
+    nc = tc.nc
+    with ExitStack() as ctx:
+        keep = ctx.enter_context(tc.tile_pool(name="keep", bufs=1))
+        work = ctx.enter_context(tc.tile_pool(name="work", bufs=3))
+        psum = ctx.enter_context(tc.psum_pool(name="psum", bufs=1))
+        ctx.enter_context(tc.manual_schedule())
+
+        def bank(kind, bufs):
+            return psum.tile([P, 512], F32, name=kind, tag=kind, bufs=bufs)
+
+        scale_v = keep.tile([P, 8], F32, name="scale_v", align_bytes=64)
+        nc.sync.dma_start(out=scale_v[:], in_=a_scale.rearrange("o (p c) -> p (o c)", p=P))
+        scale_sb = keep.tile([P, K], F32, name="scale_sb", align_bytes=64)
+        w_bf = keep.tile([P, GROUPS, 4], BF16, name="w_bf", align_bytes=64)
+        nc.scalar.dma_start(out=w_bf[:], in_=w.rearrange("(g p t) -> p g t", p=P, t=4))
+
+        ident = keep.tile([P, P], F32, name="ident", align_bytes=64)
+        make_identity(nc, ident[:])
+        jsc = keep.tile([P, NG, R], U8, name="jsc", align_bytes=64)
+        nc.gpsimd.memset(jsc[:].rearrange("p g n -> p (g n)").bitcast(I32), 0)
+        lev_sb = keep.tile([P, 4, P], F32, name="lev_sb", align_bytes=64)
+        nc.gpsimd.memset(lev_sb[:], 0.0)
+
+        warm = keep.tile([P, 1], F32, name="warm")
+        nc.scalar.activation(out=warm[:], in_=ident[:, 0:1], func=SQUARE)
+
+        a_view = a_bytes.rearrange("(g p t) k -> g p t k", p=P, t=4)
+        a8 = {}
+
+        def load_a(pair):
+            g, t0 = pair // 2, 2 * (pair % 2)
+            a8[pair] = keep.tile([P, 2, K], U8, name=f"a8_{pair}", align_bytes=64)
+            nc.sync.dma_start(out=a8[pair][:], in_=a_view[g, :, t0 : t0 + 2, :])
+
+        raw = {}
+
+        def load_rinv(h, g):
+            raw[h, g] = keep.tile([P, 4, 512], BF16, name=f"raw_{h}{g}", align_bytes=64)
+            nc.sync.dma_start(
+                out=raw[h, g][:],
+                in_=rinv.rearrange("(g p t) n -> g p t n", p=P, t=4)[g, :, :, 512 * h : 512 * (h + 1)],
+            )
+
+        jw = keep.tile([P, NG, 2 * R], U8, name="jw", align_bytes=64)
+        jsc_i = jsc[:].rearrange("p g n -> p (g n)").bitcast(I32)
+        b_sb = keep.tile([P, M], BF16, name="b_sb", align_bytes=64)
+        for item in X_DMA:
+            if item[0] == "a":
+                load_a(int(item[1:]))
+            elif item[0] == "r":
+                load_rinv(int(item[1]), int(item[2]))
+            elif item[0] == "b":
+                nc.sync.dma_start(out=b_sb[:], in_=b)
+            else:
+                nc.sync.dma_start(out=jw[:], in_=jl_words.rearrange("g p n -> p g n"))
+                for q in range(4):
+                    nc.sync.dma_start(
+                        out=jsc_i[32 * q : 32 * q + 4, :].rearrange("p (g n) -> p g n", g=NG),
+                        in_=jl_scales[:, 4 * q : 4 * q + 4, :].bitcast(I32).rearrange("g q n -> q g n"),
+                    )
+
+        w_sb = keep.tile([P, GROUPS * 4], F32, name="w_sb", align_bytes=64)
+        nc.gpsimd.tensor_copy(out=w_sb[:], in_=w_bf[:].rearrange("p g t -> p (g t)"))
+
+        rq = keep.tile([P, KG, N], U32, name="rq", align_bytes=64)
+        rs = keep.tile([P, KG, N], U8, name="rs", align_bytes=64)
+        rg = {}
+
+        def interleave_rinv(h, g, u, eng):
+            if (h, g) not in rg:
+                rg[h, g] = keep.tile([P, 512, 4], BF16, name=f"rg_{h}{g}", align_bytes=64)
+            dst = rg[h, g][:].rearrange("p (u q e) t -> p u q t e", u=2, e=2)[:, u]
+            src = raw[h, g][:].rearrange("p t (q u e) -> p u q t e", u=2, e=2)[:, u]
+            if eng == "v":
+                nc.vector.tensor_copy(out=dst, in_=src)
+            else:
+                nc.scalar.copy(out=dst, in_=src)
+            rdone.add((h, g, u))
+
+        rdone = set()
+
+        def quantize_rinv(h, g):
+            assert (h, g, 0) in rdone and (h, g, 1) in rdone
+            cols = slice(512 * h, 512 * (h + 1))
+            nc.vector.quantize_mx(
+                out=rq[:, g, cols].bitcast(FP8X4), scales=rs[:, g, cols], in_=rg[h, g][:].rearrange("p n t -> p (n t)")
+            )
+
+        ab, atr, ag, aq, asc = {}, {}, {}, {}, {}
+
+        def product(i):
+            ab[i] = work.tile([P, K], BF16, name="ab", tag="ab", bufs=4, align_bytes=64)
+            nc.vector.tensor_tensor(out=ab[i][:], in0=a8[i // 2][:, i % 2, :].bitcast(FP8), in1=scale_sb[:], op=MULT)
+
+        def transpose_a(i):
+            atr[i] = bank("tr", PTR)
+            words = ab[i][:].bitcast(F32)
+            for g in range(KG):
+                for u in range(2):
+                    s = 2 * g + u
+                    nc.tensor.transpose(
+                        atr[i][:, s * P : (s + 1) * P], words[:, 256 * g + u : 256 * (g + 1) : 2], ident[:]
+                    )
+
+        def evac_words(dst, src, eng):
+            out = dst[:].bitcast(F32).rearrange("p (g r u) -> p g r u", g=2, u=2)
+            in_ = src[:].rearrange("p (g u r) -> p g r u", g=2, u=2)
+            if eng == "v":
+                nc.vector.tensor_copy(out=out, in_=in_)
+            else:
+                nc.scalar.copy(out=out, in_=in_)
+
+        def evac_a(i, eng):
+            ag[i] = work.tile([P, 1024], BF16, name="ag", tag="ag", align_bytes=64)
+            evac_words(ag[i], atr[i], eng)
+
+        def quantize_a(i):
+            aq[i] = work.tile([P, 256], U32, name="aq", tag="aq", align_bytes=64)
+            asc[i] = work.tile([P, 256], U8, name="asc", tag="asc", align_bytes=64)
+            nc.vector.quantize_mx(out=aq[i][:].bitcast(FP8X4), scales=asc[i][:], in_=ag[i][:])
+
+        hps, hb = {}, {}
+
+        def mm_h(i, h):
+            hps[i, h] = bank("h", PH)
+            for g in range(KG):
+                rows = slice(g * P, (g + 1) * P)
+                cols = slice(512 * h, 512 * (h + 1))
+                nc.tensor.matmul_mx(
+                    out=hps[i, h][:],
+                    lhsT=aq[i][:, rows].bitcast(FP8X4),
+                    lhsT_scale=asc[i][:, rows],
+                    rhs=rq[:, g, cols].bitcast(FP8X4),
+                    rhs_scale=rs[:, g, cols],
+                    start=(g == 0),
+                    stop=(g == KG - 1),
+                )
+
+        def evac_h(i, h, eng):
+            gg, t = i // 4, i % 4
+            if gg not in hb:
+                hb[gg] = work.tile([P, 4, N], BF16, name="hb", tag="hb", align_bytes=64)
+            dst = hb[gg][:, t, 512 * h : 512 * (h + 1)]
+            if eng == "v":
+                nc.vector.tensor_scalar(out=dst, in0=hps[i, h][:], scalar1=w_sb[:, i : i + 1], scalar2=None, op0=MULT)
+            else:
+                nc.scalar.activation(out=dst, in_=hps[i, h][:], func=COPY, scale=w_sb[:, i : i + 1])
+
+        htr, htg, hq, hs = {}, {}, {}, {}
+
+        def transpose_h(i):
+            htr[i] = bank("tr", PTR)
+            words = hb[i // 4][:, i % 4, :].bitcast(F32)
+            for s in range(4):
+                nc.tensor.transpose(htr[i][:, s * P : (s + 1) * P], words[:, s * P : (s + 1) * P], ident[:])
+
+        def evac_ht(i, eng):
+            htg[i] = work.tile([P, 1024], BF16, name="htg", tag="htg", align_bytes=64)
+            evac_words(htg[i], htr[i], eng)
+
+        def quantize_ht(i):
+            hq[i] = work.tile([P, 256], U32, name="hq", tag="hq", align_bytes=64)
+            hs[i] = work.tile([P, 256], U8, name="hs", tag="hs", align_bytes=64)
+            nc.vector.quantize_mx(out=hq[i][:].bitcast(FP8X4), scales=hs[i][:], in_=htg[i][:])
+
+        yps = {}
+
+        def mm_y(i):
+            yps[i] = bank("y", PY)
+            for g in range(NG):
+                rows = slice(g * P, (g + 1) * P)
+                nc.tensor.matmul_mx(
+                    out=yps[i][:],
+                    lhsT=hq[i][:, rows].bitcast(FP8X4),
+                    lhsT_scale=hs[i][:, rows],
+                    rhs=jw[:, g, :].bitcast(FP4X4),
+                    rhs_scale=jsc[:, g, :],
+                    start=(g == 0),
+                    stop=(g == NG - 1),
+                )
+
+        y_view = y.rearrange("(g p t) n -> g t p n", p=P, t=4)
+
+        def evac_y(i, eng):
+            y_sb = work.tile([P, R], F32, name="y_sb", tag="y_sb", align_bytes=64)
+            if eng == "v":
+                nc.vector.tensor_copy(out=y_sb[:], in_=yps[i][:])
+            else:
+                nc.scalar.copy(out=y_sb[:], in_=yps[i][:])
+            nc.sync.dma_start(out=y_view[i // 4, i % 4], in_=y_sb[:])
+
+        def lev_y(i):
+            sq = work.tile([P, R], BF16, name="sq", tag="sq", align_bytes=64)
+            nc.scalar.activation(
+                out=sq[:], in_=yps[i][:], func=SQUARE, scale=R**-0.5,
+                accum_out=lev_sb[:, i % 4, i // 4 : i // 4 + 1],
+            )
+
+        cg, cq, cs = {}, {}, {}
+
+        def interleave_c(gg, h):
+            cg[gg, h] = work.tile([P, 512, 4], BF16, name="cg", tag="cg", align_bytes=64)
+            nc.vector.tensor_copy(
+                out=cg[gg, h][:].rearrange("p (c i) t -> p c t i", i=4),
+                in_=hb[gg][:, :, 512 * h : 512 * (h + 1)].rearrange("p t (c i) -> p c t i", i=4),
+            )
+
+        def quantize_c(gg, h):
+            cq[gg, h] = keep.tile([P, 512], U32, name=f"cq_{gg}{h}", align_bytes=64)
+            cs[gg, h] = keep.tile([P, 512], U8, name=f"cs_{gg}{h}", align_bytes=64)
+            nc.vector.quantize_mx(
+                out=cq[gg, h][:].bitcast(FP8X4), scales=cs[gg, h][:], in_=cg[gg, h][:].rearrange("p n t -> p (n t)")
+            )
+
+        btr = {}
+        bg = keep.tile([P, 6, P, 4], BF16, name="bg", align_bytes=64)
+        bq = keep.tile([P, 6 * P], U32, name="bq", align_bytes=64)
+        bs = keep.tile([P, 6 * P], U8, name="bs", align_bytes=64)
+
+        def transpose_b(j):
+            btr[j] = bank("tr", PTR)
+            words = b_sb[:].bitcast(F32)
+            for s in range(4):
+                g, u = 2 * j + s // 2, s % 2
+                nc.tensor.transpose(btr[j][:, s * P : (s + 1) * P], words[:, 256 * g + u : 256 * (g + 1) : 2], ident[:])
+
+        def evac_b(j, eng):
+            out = bg[:, 2 * j : 2 * j + 2].rearrange("p g r t -> p (g r t)").bitcast(F32).rearrange(
+                "p (g r u) -> p g r u", g=2, u=2
+            )
+            in_ = btr[j][:].rearrange("p (g u r) -> p g r u", g=2, u=2)
+            if eng == "v":
+                nc.vector.tensor_copy(out=out, in_=in_)
+            else:
+                nc.scalar.copy(out=out, in_=in_)
+
+        def quantize_b(j):
+            cols = slice(256 * j, 256 * (j + 1))
+            nc.vector.quantize_mx(
+                out=bq[:, cols].bitcast(FP8X4), scales=bs[:, cols],
+                in_=bg[:, 2 * j : 2 * j + 2].rearrange("p g r t -> p (g r t)"),
+            )
+
+        cps = {}
+
+        def mm_c(gg, h):
+            if gg == 0:
+                cps[h] = bank("h", PH)
+            rows = slice(gg * P, (gg + 1) * P)
+            nc.tensor.matmul_mx(
+                out=cps[h][:],
+                lhsT=bq[:, rows].bitcast(FP8X4),
+                lhsT_scale=bs[:, rows],
+                rhs=cq[gg, h][:].bitcast(FP8X4),
+                rhs_scale=cs[gg, h][:],
+                start=(gg == 0),
+                stop=(gg == GROUPS - 1),
+            )
+
+        def evac_c(h, eng):
+            c_sb = work.tile([P, 512], F32, name="c_sb", tag="c_sb", align_bytes=64)
+            out = c_sb[:].rearrange("p (q u e) -> p q u e", u=2, e=2)
+            in_ = cps[h][:].rearrange("p (u q e) -> p q u e", u=2, e=2)
+            if eng == "v":
+                nc.vector.tensor_copy(out=out, in_=in_)
+            else:
+                nc.scalar.copy(out=out, in_=in_)
+            nc.sync.dma_start(out=c[:, 512 * h : 512 * (h + 1)], in_=c_sb[:])
+
+        def eng(rule, i):
+            pattern, head, tail = rule
+            return "s" if i < head else "v" if i >= tail else pattern[i % len(pattern)]
+
+        for half in range(2):
+            sps = bank("tr", PTR)
+            for j in range(4):
+                c0 = 4 * half + j
+                nc.tensor.transpose(sps[:, j * P : (j + 1) * P], scale_v[:, c0 : c0 + 1].to_broadcast([P, P]), ident[:])
+            out = scale_sb[:].rearrange("p (k c) -> p k c", c=8)[:, :, 4 * half : 4 * half + 4]
+            in_ = sps[:].rearrange("p (c k) -> p k c", c=4)
+            if X_SC[half] == "v":
+                nc.vector.tensor_copy(out=out, in_=in_)
+            else:
+                nc.scalar.copy(out=out, in_=in_)
+        done = set()
+
+        def run(tok, i):
+            if tok == "P":
+                product(i)
+            elif tok == "TA":
+                transpose_a(i)
+            elif tok == "EA":
+                evac_a(i, eng(X_EA, i))
+            elif tok == "QA":
+                quantize_a(i)
+            elif tok == "H0" or tok == "H1":
+                mm_h(i, int(tok[1]))
+            elif tok == "E0" or tok == "E1":
+                evac_h(i, int(tok[1]), eng(X_EE, 2 * i + int(tok[1])))
+                done.add((i, tok))
+            elif tok == "TH":
+                assert (i, "E0") in done and (i, "E1") in done
+                transpose_h(i)
+            elif tok == "EH":
+                evac_ht(i, eng(X_EH, i))
+            elif tok == "QH":
+                quantize_ht(i)
+            elif tok == "Y":
+                mm_y(i)
+            elif tok == "EY":
+                evac_y(i, eng(X_EY, i))
+            elif tok == "LV":
+                lev_y(i)
+            elif tok[:2] in ("IC", "QC"):
+                if i % 4 == 3:
+                    assert (i, "E0") in done and (i, "E1") in done
+                    (interleave_c if tok[0] == "I" else quantize_c)(i // 4, int(tok[2]))
+                    if tok == "QC1":
+                        mm_c_ready.append(i // 4)
+
+        mm_c_ready = []
+        rinv_todo = list(RINV)
+        cdone = 0
+        for s in range(-2, TILES + 14):
+            for tok, lag, per in ORDER:
+                if tok == "R":
+                    for x in [x for x in rinv_todo if x[0] == s + lag]:
+                        if x[1] == "I":
+                            interleave_rinv(x[2], x[3], x[4], x[5])
+                        else:
+                            quantize_rinv(x[2], x[3])
+                elif tok == "B":
+                    j = s - BSTART
+                    if 0 <= j < 3 * 2:
+                        if j % 2 == 0:
+                            transpose_b(j // 2)
+                            evac_b(j // 2, BENG)
+                        else:
+                            quantize_b(j // 2)
+                else:
+                    tiles = [s - lag] if per == 1 else ([s - lag - 1, s - lag] if s % 2 else [])
+                    for i in tiles:
+                        if 0 <= i < TILES:
+                            run(tok, i)
+            if s >= CSTART and cdone < len(mm_c_ready):
+                for gg in mm_c_ready[cdone:]:
+                    for h in range(2):
+                        mm_c(gg, h)
+                        if gg == GROUPS - 1:
+                            evac_c(h, CENG[h])
+                cdone = len(mm_c_ready)
+
+        lps = bank("tr", PTR)
+        for t in range(4):
+            nc.tensor.transpose(lps[:, t * P : (t + 1) * P], lev_sb[:, t, :], ident[:])
+        lev_rows = keep.tile([P, 512], F32, name="lev_rows", align_bytes=64)
+        nc.vector.tensor_copy(
+            out=lev_rows[:GROUPS, :].rearrange("g (p t) -> g p t", t=4),
+            in_=lps[:GROUPS, :].rearrange("g (t p) -> g p t", t=4),
+        )
+        nc.sync.dma_start(out=lev.rearrange("(g m) -> g m", g=GROUPS), in_=lev_rows[:GROUPS, :])

@@ -19,16 +19,18 @@ COPY = mybir.ActivationFunctionType.Copy
 SQUARE = mybir.ActivationFunctionType.Square
 
 P = 128
-X_DMA = ["a0", "r00", "r11", "r01", "r10", "a1", "a2", "j", "a4", "a3", "a7", "a6", "a5", "a8", "a9", "b", "a10", "a11"]
+X_DMA = ["r00", "a0", "r01", "r10", "a1", "r11", "a6", "a2", "a3", "j", "a4", "a5", "a7", "a10", "a8", "b", "a9", "a11"]
 X_SC = "vs"
-PTR, PH, PY = 2, 3, 3
-ORDER = [("TA", 0, 1), ("R", 0, 1), ("IC0", 2, 1), ("TH", 2, 1), ("EA", 0, 1), ("EY", 4, 1), ("H0", 1, 1), ("EH", 2, 1), ("H1", 1, 1), ("P", -2, 1), ("E0", 1, 1), ("QA", 0, 1), ("QC1", 4, 1), ("QC0", 3, 1), ("QH", 2, 1), ("E1", 1, 1), ("B", 0, 1), ("Y", 3, 1), ("LV", 5, 1), ("IC1", 3, 1)]
-RINV = [(1, "I", 0, 1, 0, "s"), (1, "Q", 0, 1), (-2, "I", 0, 0, 1, "s"), (1, "Q", 1, 1), (-2, "I", 1, 1, 0, "s"), (-1, "Q", 0, 0), (0, "I", 1, 0, 1, "s"), (-2, "I", 0, 0, 0, "v"), (0, "I", 1, 0, 0, "v"), (0, "Q", 1, 0), (-1, "I", 1, 1, 1, "v"), (-1, "I", 0, 1, 1, "v")]
-X_EA = ("sssv", 3, 26)
-X_EH = ("ssss", 1, 38)
-X_EY = ("vvss", 0, 18)
-X_EE = ("ssssssss", 5, 50)
-BSTART, BENG, CSTART, CENG = 16, "s", 31, "sv"
+X_A2 = "1111"
+PTR, PH, PY = 4, 2, 2
+ORDER = [("P1", -1), ("BQ", 3), ("TA1", 0), ("TH0", 2), ("TA0", 0), ("EH0", 2), ("HM00", 1), ("EA0", 0), ("HM10", 1), ("HE00", 1), ("EA1", 0), ("HE10", 1), ("TH1", 2), ("P0", -1), ("HM01", 1), ("HM11", 1), ("IC0", 2), ("IC1", 2), ("QA0", 1), ("EH1", 2), ("HE01", 1), ("HE11", 1), ("QH0", -1), ("QA1", 0), ("Y0", 3), ("R", 0), ("Y1", 3), ("C", 0), ("EY0", 3), ("QH1", 2), ("QC1", 2), ("W1", -4), ("LV0", 3), ("EY1", 3), ("QC0", 2), ("LV1", 3), ("B", 0), ("W0", 0)]
+SINGLE = ()
+RINV = [(-1, "I", 0, 1, 0, "v"), (-1, "Q", 0, 0), (0, "I", 1, 0, 0, "v"), (-1, "I", 1, 0, 1, "s"), (-2, "I", 0, 0, 1, "v"), (0, "I", 1, 1, 0, "s"), (-2, "I", 0, 0, 0, "s"), (0, "I", 1, 1, 1, "s"), (0, "Q", 0, 1), (-2, "I", 0, 1, 1, "s"), (0, "Q", 1, 0), (0, "Q", 1, 1)]
+X_EA = ("svsv", 4, 32)
+X_EH = ("vsss", 3, 31)
+X_EY = ("ssvs", 5, 22)
+X_EE = ("ssssssss", 2, 46)
+BSTART, BENG, CSTART, CENG = 7, "s", 13, "sv"
 GROUPS = M // 512
 TILES = M // P
 KG = K // 512
@@ -50,6 +52,8 @@ def tile_weighted_leverage_sketch_s8_kernel(
 
         scale_v = keep.tile([P, 8], F32, name="scale_v", align_bytes=64)
         nc.sync.dma_start(out=scale_v[:], in_=a_scale.rearrange("o (p c) -> p (o c)", p=P))
+        scale_p = keep.tile([P, KG, 2, 2], F32, name="scale_p", align_bytes=64)
+        nc.scalar.dma_start(out=scale_p[:].rearrange("p g u e -> p g (u e)"), in_=a_scale.rearrange("o (g p t) -> p (o g) t", p=P, t=4))
         scale_sb = keep.tile([P, K], F32, name="scale_sb", align_bytes=64)
         w_bf = keep.tile([P, GROUPS, 4], BF16, name="w_bf", align_bytes=64)
         nc.scalar.dma_start(out=w_bf[:], in_=w.rearrange("(g p t) -> p g t", p=P, t=4))
@@ -126,11 +130,26 @@ def tile_weighted_leverage_sketch_s8_kernel(
                 out=rq[:, g, cols].bitcast(FP8X4), scales=rs[:, g, cols], in_=rg[h, g][:].rearrange("p n t -> p (n t)")
             )
 
+        ag_pair, aq_pair, as_pair, htg_pair, hq_pair, hs_pair = {}, {}, {}, {}, {}, {}
         ab, atr, ag, aq, asc = {}, {}, {}, {}, {}
 
         def product(i):
             ab[i] = work.tile([P, K], BF16, name="ab", tag="ab", bufs=4, align_bytes=64)
             nc.vector.tensor_tensor(out=ab[i][:], in0=a8[i // 2][:, i % 2, :].bitcast(FP8), in1=scale_sb[:], op=MULT)
+
+        def widen(i):
+            ab[i] = work.tile([P, K], BF16, name="ab", tag="ab", bufs=4, align_bytes=64)
+            nc.gpsimd.tensor_copy(out=ab[i][:], in_=a8[i // 2][:, i % 2, :].bitcast(FP8))
+
+        def evac_scale(i):
+            in_ = atr[i][:].bitcast(BF16)
+            for g in range(KG):
+                nc.vector.tensor_tensor(
+                    out=ag[i][:, 512 * g : 512 * (g + 1)].rearrange("p (r u e) -> p r u e", u=2, e=2),
+                    in0=in_[:, 512 * g : 512 * (g + 1)].rearrange("p (u r e) -> p r u e", u=2, e=2),
+                    in1=scale_p[:, g].unsqueeze(1).to_broadcast([P, P, 2, 2]),
+                    op=MULT,
+                )
 
         def transpose_a(i):
             atr[i] = bank("tr", PTR)
@@ -143,7 +162,7 @@ def tile_weighted_leverage_sketch_s8_kernel(
                     )
 
         def evac_words(dst, src, eng):
-            out = dst[:].bitcast(F32).rearrange("p (g r u) -> p g r u", g=2, u=2)
+            out = dst.bitcast(F32).rearrange("p (g r u) -> p g r u", g=2, u=2)
             in_ = src[:].rearrange("p (g u r) -> p g r u", g=2, u=2)
             if eng == "v":
                 nc.vector.tensor_copy(out=out, in_=in_)
@@ -151,13 +170,32 @@ def tile_weighted_leverage_sketch_s8_kernel(
                 nc.scalar.copy(out=out, in_=in_)
 
         def evac_a(i, eng):
-            ag[i] = work.tile([P, 1024], BF16, name="ag", tag="ag", align_bytes=64)
-            evac_words(ag[i], atr[i], eng)
+            if i % 2 == 0:
+                ag_pair[i // 2] = work.tile([P, 2, 1024], BF16, name="ag", tag="ag", align_bytes=64)
+            ag[i] = ag_pair[i // 2][:, i % 2]
+            if X_A2[i % len(X_A2)] == "2":
+                evac_scale(i)
+            else:
+                evac_words(ag[i], atr[i], eng)
 
-        def quantize_a(i):
-            aq[i] = work.tile([P, 256], U32, name="aq", tag="aq", align_bytes=64)
-            asc[i] = work.tile([P, 256], U8, name="asc", tag="asc", align_bytes=64)
-            nc.vector.quantize_mx(out=aq[i][:].bitcast(FP8X4), scales=asc[i][:], in_=ag[i][:])
+        def quantize_pair(tiles, pair_codes, pair_scales, grouped, codes, scales, kind):
+            for i in tiles:
+                if i % 2 == 0:
+                    pair_codes[i // 2] = work.tile([P, 512], U32, name=kind + "q", tag=kind + "q", align_bytes=64)
+                    pair_scales[i // 2] = work.tile([P, 512], U8, name=kind + "s", tag=kind + "s", align_bytes=64)
+                codes[i] = pair_codes[i // 2][:, 256 * (i % 2) : 256 * (i % 2) + 256]
+                scales[i] = pair_scales[i // 2][:, 256 * (i % 2) : 256 * (i % 2) + 256]
+            pair, lo, hi = tiles[0] // 2, tiles[0] % 2, tiles[-1] % 2 + 1
+            nc.vector.quantize_mx(
+                out=pair_codes[pair][:, 256 * lo : 256 * hi].bitcast(FP8X4),
+                scales=pair_scales[pair][:, 256 * lo : 256 * hi],
+                in_=grouped[pair][:, lo:hi].rearrange("p i c -> p (i c)"),
+            )
+
+        def quantize_a(tiles):
+            for i in tiles:
+                assert i in ag
+            quantize_pair(tiles, aq_pair, as_pair, ag_pair, aq, asc, "a")
 
         hps, hb = {}, {}
 
@@ -195,13 +233,15 @@ def tile_weighted_leverage_sketch_s8_kernel(
                 nc.tensor.transpose(htr[i][:, s * P : (s + 1) * P], words[:, s * P : (s + 1) * P], ident[:])
 
         def evac_ht(i, eng):
-            htg[i] = work.tile([P, 1024], BF16, name="htg", tag="htg", align_bytes=64)
+            if i % 2 == 0:
+                htg_pair[i // 2] = work.tile([P, 2, 1024], BF16, name="htg", tag="htg", align_bytes=64)
+            htg[i] = htg_pair[i // 2][:, i % 2]
             evac_words(htg[i], htr[i], eng)
 
-        def quantize_ht(i):
-            hq[i] = work.tile([P, 256], U32, name="hq", tag="hq", align_bytes=64)
-            hs[i] = work.tile([P, 256], U8, name="hs", tag="hs", align_bytes=64)
-            nc.vector.quantize_mx(out=hq[i][:].bitcast(FP8X4), scales=hs[i][:], in_=htg[i][:])
+        def quantize_ht(tiles):
+            for i in tiles:
+                assert i in htg
+            quantize_pair(tiles, hq_pair, hs_pair, htg_pair, hq, hs, "h")
 
         yps = {}
 
@@ -323,46 +363,58 @@ def tile_weighted_leverage_sketch_s8_kernel(
             else:
                 nc.scalar.copy(out=out, in_=in_)
         done = set()
-
-        def run(tok, i):
-            if tok == "P":
-                product(i)
-            elif tok == "TA":
-                transpose_a(i)
-            elif tok == "EA":
-                evac_a(i, eng(X_EA, i))
-            elif tok == "QA":
-                quantize_a(i)
-            elif tok == "H0" or tok == "H1":
-                mm_h(i, int(tok[1]))
-            elif tok == "E0" or tok == "E1":
-                evac_h(i, int(tok[1]), eng(X_EE, 2 * i + int(tok[1])))
-                done.add((i, tok))
-            elif tok == "TH":
-                assert (i, "E0") in done and (i, "E1") in done
-                transpose_h(i)
-            elif tok == "EH":
-                evac_ht(i, eng(X_EH, i))
-            elif tok == "QH":
-                quantize_ht(i)
-            elif tok == "Y":
-                mm_y(i)
-            elif tok == "EY":
-                evac_y(i, eng(X_EY, i))
-            elif tok == "LV":
-                lev_y(i)
-            elif tok[:2] in ("IC", "QC"):
-                if i % 4 == 3:
-                    assert (i, "E0") in done and (i, "E1") in done
-                    (interleave_c if tok[0] == "I" else quantize_c)(i // 4, int(tok[2]))
-                    if tok == "QC1":
-                        mm_c_ready.append(i // 4)
-
         mm_c_ready = []
+
+        def run(tok, pair):
+            i = 2 * pair + int(tok[-1])
+            h = int(tok[-2]) if tok[-2] in "01" else 0
+            k = tok[:2]
+            if k == "P0" or k == "P1":
+                if X_A2[i % len(X_A2)] == "1":
+                    product(i)
+            elif k == "W0" or k == "W1":
+                if X_A2[i % len(X_A2)] == "2":
+                    widen(i)
+            elif k == "TA":
+                transpose_a(i)
+            elif k == "EA":
+                evac_a(i, eng(X_EA, i))
+            elif k == "QA" or k == "QH":
+                q = quantize_a if k == "QA" else quantize_ht
+                if pair in SINGLE:
+                    q([i])
+                elif i % 2 == 1:
+                    q([i - 1, i])
+            elif k == "HM":
+                mm_h(i, h)
+            elif k == "HE":
+                evac_h(i, h, eng(X_EE, 2 * i + h))
+                done.add((i, h))
+            elif k == "TH":
+                assert (i, 0) in done and (i, 1) in done
+                transpose_h(i)
+            elif k == "EH":
+                evac_ht(i, eng(X_EH, i))
+            elif k == "Y0" or k == "Y1":
+                mm_y(i)
+            elif k == "EY":
+                evac_y(i, eng(X_EY, i))
+            elif k == "LV":
+                lev_y(i)
+            elif k == "IC" or k == "QC":
+                if pair % 2 == 1:
+                    h = int(tok[-1])
+                    for j in range(4):
+                        assert (2 * pair + 1 - j, h) in done
+                    (interleave_c if k == "IC" else quantize_c)(pair // 2, h)
+                    if k == "QC":
+                        qdone.add((pair // 2, h))
+
+        qdone = set()
         rinv_todo = list(RINV)
         cdone = 0
-        for s in range(-2, TILES + 14):
-            for tok, lag, per in ORDER:
+        for s in range(-2, TILES // 2 + 8):
+            for tok, lag in ORDER:
                 if tok == "R":
                     for x in [x for x in rinv_todo if x[0] == s + lag]:
                         if x[1] == "I":
@@ -371,24 +423,23 @@ def tile_weighted_leverage_sketch_s8_kernel(
                             quantize_rinv(x[2], x[3])
                 elif tok == "B":
                     j = s - BSTART
-                    if 0 <= j < 3 * 2:
-                        if j % 2 == 0:
-                            transpose_b(j // 2)
-                            evac_b(j // 2, BENG)
-                        else:
-                            quantize_b(j // 2)
-                else:
-                    tiles = [s - lag] if per == 1 else ([s - lag - 1, s - lag] if s % 2 else [])
-                    for i in tiles:
-                        if 0 <= i < TILES:
-                            run(tok, i)
-            if s >= CSTART and cdone < len(mm_c_ready):
-                for gg in mm_c_ready[cdone:]:
-                    for h in range(2):
-                        mm_c(gg, h)
-                        if gg == GROUPS - 1:
-                            evac_c(h, CENG[h])
-                cdone = len(mm_c_ready)
+                    if 0 <= j < 3:
+                        transpose_b(j)
+                        evac_b(j, BENG)
+                elif tok == "BQ":
+                    j = s - BSTART - lag
+                    if 0 <= j < 3:
+                        quantize_b(j)
+                elif tok == "C":
+                    while s >= CSTART and cdone < GROUPS and (cdone, 0) in qdone and (cdone, 1) in qdone:
+                        for h in range(2):
+                            mm_c(cdone, h)
+                        cdone += 1
+                elif 0 <= s - lag < TILES // 2:
+                    run(tok, s - lag)
+        assert cdone == GROUPS
+        for h in range(2):
+            evac_c(h, CENG[h])
 
         lps = bank("tr", PTR)
         for t in range(4):

@@ -19,18 +19,18 @@ COPY = mybir.ActivationFunctionType.Copy
 SQUARE = mybir.ActivationFunctionType.Square
 
 P = 128
-X_DMA = ["r00", "a0", "r01", "r10", "a1", "r11", "a6", "a2", "a3", "j", "a4", "a5", "a7", "a10", "a8", "b", "a9", "a11"]
-X_SC = "vs"
-X_A2 = "1111"
-PTR, PH, PY = 4, 2, 2
-ORDER = [("P1", -1), ("BQ", 3), ("TA1", 0), ("TH0", 2), ("TA0", 0), ("EH0", 2), ("HM00", 1), ("EA0", 0), ("HM10", 1), ("HE00", 1), ("EA1", 0), ("HE10", 1), ("TH1", 2), ("P0", -1), ("HM01", 1), ("HM11", 1), ("IC0", 2), ("IC1", 2), ("QA0", 1), ("EH1", 2), ("HE01", 1), ("HE11", 1), ("QH0", -1), ("QA1", 0), ("Y0", 3), ("R", 0), ("Y1", 3), ("C", 0), ("EY0", 3), ("QH1", 2), ("QC1", 2), ("W1", -4), ("LV0", 3), ("EY1", 3), ("QC0", 2), ("LV1", 3), ("B", 0), ("W0", 0)]
-SINGLE = ()
-RINV = [(-1, "I", 0, 1, 0, "v"), (-1, "Q", 0, 0), (0, "I", 1, 0, 0, "v"), (-1, "I", 1, 0, 1, "s"), (-2, "I", 0, 0, 1, "v"), (0, "I", 1, 1, 0, "s"), (-2, "I", 0, 0, 0, "s"), (0, "I", 1, 1, 1, "s"), (0, "Q", 0, 1), (-2, "I", 0, 1, 1, "s"), (0, "Q", 1, 0), (0, "Q", 1, 1)]
-X_EA = ("svsv", 4, 32)
-X_EH = ("vsss", 3, 31)
-X_EY = ("ssvs", 5, 22)
-X_EE = ("ssssssss", 2, 46)
-BSTART, BENG, CSTART, CENG = 7, "s", 13, "sv"
+X_DMA = ["a0", "r00", "r01", "a1", "r10", "r11", "a2", "j", "a3", "a4", "a5", "a6", "a7", "b", "a8", "a9", "a10", "a11"]
+X_SC = "ss"
+X_A2 = ("1111", 0, 24)
+MODE = 2
+PTR, PH, PY = 3, 3, 2
+ORDER = [("EY1", 6, 1), ("TA0", 0, 1), ("QH", 5, 1), ("P", -53, 1), ("TH0", 3, 1), ("F11", 2, 1), ("QA", 1, 1), ("EH1", 4, 1), ("IC1", 6, 1), ("LV1", 6, 1), ("B", 0, 1), ("IC0", 3, 1), ("R", 0, 1), ("MS", -1, 1), ("F00", 2, 1), ("EH0", 3, 1), ("Y0", 5, 1), ("QC0", 4, 1), ("BQ", 1, 1), ("TA1", 0, 1), ("M01", 1, 1), ("M10", 1, 1), ("EY0", 5, 1), ("EA0", 0, 1), ("LV0", 5, 1), ("EA1", 0, 1), ("Y1", 5, 1), ("F01", 1, 1), ("QC1", 8, 1), ("M11", 1, 1), ("M00", 1, 1), ("TH1", 3, 1), ("F10", 1, 1), ("W0", -1, 1), ("W1", -1, 1)]
+RINV = [(-3, "I", 0, 0, 1, "s"), (-2, "I", 0, 1, 1, "s"), (1, "I", 1, 1, 1, "v"), (1, "Q", 0, 0), (1, "Q", 0, 1), (-2, "I", 0, 0, 0, "s"), (1, "Q", 1, 0), (-2, "I", 1, 0, 1, "s"), (1, "Q", 1, 1), (-2, "I", 1, 0, 0, "s"), (0, "I", 0, 1, 0, "v"), (-2, "I", 1, 1, 0, "s")]
+X_EA = ("vvvv", 3, 21)
+X_EH = ("ssss", 12, 23)
+X_EY = ("ssss", 1, 24)
+X_EE = ("vsssssss", 12, 44)
+BSTART, BENG, CSTART, CENG = 13, "s", -58, "vv"
 GROUPS = M // 512
 TILES = M // P
 KG = K // 512
@@ -54,7 +54,7 @@ def tile_weighted_leverage_sketch_s8_kernel(
         nc.sync.dma_start(out=scale_v[:], in_=a_scale.rearrange("o (p c) -> p (o c)", p=P))
         scale_p = keep.tile([P, KG, 2, 2], F32, name="scale_p", align_bytes=64)
         nc.scalar.dma_start(out=scale_p[:].rearrange("p g u e -> p g (u e)"), in_=a_scale.rearrange("o (g p t) -> p (o g) t", p=P, t=4))
-        scale_sb = keep.tile([P, K], F32, name="scale_sb", align_bytes=64)
+        scale_sb = keep.tile([P, 2 * K if MODE == 1 else 8], F32, name="scale_sb", align_bytes=64)
         w_bf = keep.tile([P, GROUPS, 4], BF16, name="w_bf", align_bytes=64)
         nc.scalar.dma_start(out=w_bf[:], in_=w.rearrange("(g p t) -> p g t", p=P, t=4))
 
@@ -133,32 +133,31 @@ def tile_weighted_leverage_sketch_s8_kernel(
         ag_pair, aq_pair, as_pair, htg_pair, hq_pair, hs_pair = {}, {}, {}, {}, {}, {}
         ab, atr, ag, aq, asc = {}, {}, {}, {}, {}
 
-        def product(i):
-            ab[i] = work.tile([P, K], BF16, name="ab", tag="ab", bufs=4, align_bytes=64)
-            nc.vector.tensor_tensor(out=ab[i][:], in0=a8[i // 2][:, i % 2, :].bitcast(FP8), in1=scale_sb[:], op=MULT)
+        def product(pair):
+            ab[pair] = work.tile([P, 2, K], BF16, name="ab", tag="ab", align_bytes=64)
+            nc.vector.tensor_tensor(
+                out=ab[pair][:].rearrange("p i k -> p (i k)"),
+                in0=a8[pair][:].rearrange("p i k -> p (i k)").bitcast(FP8),
+                in1=scale_sb[:],
+                op=MULT,
+            )
 
-        def widen(i):
-            ab[i] = work.tile([P, K], BF16, name="ab", tag="ab", bufs=4, align_bytes=64)
-            nc.gpsimd.tensor_copy(out=ab[i][:], in_=a8[i // 2][:, i % 2, :].bitcast(FP8))
+        def claim(pair):
+            ab[pair] = work.tile([P, 2, K], BF16, name="ab", tag="ab", align_bytes=64)
+            nc.vector.memset(ab[pair][:, :, 0:2], 0.0)
 
-        def evac_scale(i):
-            in_ = atr[i][:].bitcast(BF16)
-            for g in range(KG):
-                nc.vector.tensor_tensor(
-                    out=ag[i][:, 512 * g : 512 * (g + 1)].rearrange("p (r u e) -> p r u e", u=2, e=2),
-                    in0=in_[:, 512 * g : 512 * (g + 1)].rearrange("p (u r e) -> p r u e", u=2, e=2),
-                    in1=scale_p[:, g].unsqueeze(1).to_broadcast([P, P, 2, 2]),
-                    op=MULT,
-                )
+        def widen(pair, i):
+            assert pair in ab
+            nc.gpsimd.tensor_copy(out=ab[pair][:, i, :], in_=a8[pair][:, i, :].bitcast(FP8))
 
-        def transpose_a(i):
-            atr[i] = bank("tr", PTR)
-            words = ab[i][:].bitcast(F32)
-            for g in range(KG):
-                for u in range(2):
-                    s = 2 * g + u
+        def transpose_a(pair, g):
+            atr[pair, g] = bank("tr", PTR)
+            for u in range(2):
+                for i in range(2):
+                    s = 2 * u + i
+                    words = ab[pair][:, i, :].bitcast(F32)
                     nc.tensor.transpose(
-                        atr[i][:, s * P : (s + 1) * P], words[:, 256 * g + u : 256 * (g + 1) : 2], ident[:]
+                        atr[pair, g][:, s * P : (s + 1) * P], words[:, 256 * g + u : 256 * (g + 1) : 2], ident[:]
                     )
 
         def evac_words(dst, src, eng):
@@ -169,45 +168,42 @@ def tile_weighted_leverage_sketch_s8_kernel(
             else:
                 nc.scalar.copy(out=out, in_=in_)
 
-        def evac_a(i, eng):
-            if i % 2 == 0:
-                ag_pair[i // 2] = work.tile([P, 2, 1024], BF16, name="ag", tag="ag", align_bytes=64)
-            ag[i] = ag_pair[i // 2][:, i % 2]
-            if X_A2[i % len(X_A2)] == "2":
-                evac_scale(i)
+        def evac_a(pair, g):
+            if pair not in ag:
+                ag[pair] = work.tile([P, KG, 1024], BF16, name="ag", tag="ag", align_bytes=64)
+            if MODE == 2:
+                nc.vector.tensor_tensor(
+                    out=ag[pair][:, g].rearrange("p (c u e) -> p c u e", u=2, e=2),
+                    in0=atr[pair, g][:].bitcast(BF16).rearrange("p (u c e) -> p c u e", u=2, e=2),
+                    in1=scale_p[:, g].unsqueeze(1).to_broadcast([P, 2 * P, 2, 2]),
+                    op=MULT,
+                )
             else:
-                evac_words(ag[i], atr[i], eng)
+                out = ag[pair][:, g].bitcast(F32).rearrange("p (c u) -> p c u", u=2)
+                in_ = atr[pair, g][:].rearrange("p (u c) -> p c u", u=2)
+                if eng(X_EA, 2 * pair + g) == "v":
+                    nc.vector.tensor_copy(out=out, in_=in_)
+                else:
+                    nc.scalar.copy(out=out, in_=in_)
 
-        def quantize_pair(tiles, pair_codes, pair_scales, grouped, codes, scales, kind):
-            for i in tiles:
-                if i % 2 == 0:
-                    pair_codes[i // 2] = work.tile([P, 512], U32, name=kind + "q", tag=kind + "q", align_bytes=64)
-                    pair_scales[i // 2] = work.tile([P, 512], U8, name=kind + "s", tag=kind + "s", align_bytes=64)
-                codes[i] = pair_codes[i // 2][:, 256 * (i % 2) : 256 * (i % 2) + 256]
-                scales[i] = pair_scales[i // 2][:, 256 * (i % 2) : 256 * (i % 2) + 256]
-            pair, lo, hi = tiles[0] // 2, tiles[0] % 2, tiles[-1] % 2 + 1
-            nc.vector.quantize_mx(
-                out=pair_codes[pair][:, 256 * lo : 256 * hi].bitcast(FP8X4),
-                scales=pair_scales[pair][:, 256 * lo : 256 * hi],
-                in_=grouped[pair][:, lo:hi].rearrange("p i c -> p (i c)"),
-            )
-
-        def quantize_a(tiles):
-            for i in tiles:
-                assert i in ag
-            quantize_pair(tiles, aq_pair, as_pair, ag_pair, aq, asc, "a")
+        def quantize_a(pair):
+            q = work.tile([P, 512], U32, name="aq", tag="aq", align_bytes=64)
+            s = work.tile([P, 512], U8, name="asc", tag="asc", align_bytes=64)
+            nc.vector.quantize_mx(out=q[:].bitcast(FP8X4), scales=s[:], in_=ag[pair][:].rearrange("p g c -> p (g c)"))
+            for i in range(2):
+                aq[2 * pair + i] = q[:].rearrange("p (g i m) -> p i g m", g=KG, i=2)[:, i]
+                asc[2 * pair + i] = s[:].rearrange("p (g i m) -> p i g m", g=KG, i=2)[:, i]
 
         hps, hb = {}, {}
 
         def mm_h(i, h):
             hps[i, h] = bank("h", PH)
             for g in range(KG):
-                rows = slice(g * P, (g + 1) * P)
                 cols = slice(512 * h, 512 * (h + 1))
                 nc.tensor.matmul_mx(
                     out=hps[i, h][:],
-                    lhsT=aq[i][:, rows].bitcast(FP8X4),
-                    lhsT_scale=asc[i][:, rows],
+                    lhsT=aq[i][:, g].bitcast(FP8X4),
+                    lhsT_scale=asc[i][:, g],
                     rhs=rq[:, g, cols].bitcast(FP8X4),
                     rhs_scale=rs[:, g, cols],
                     start=(g == 0),
@@ -233,15 +229,22 @@ def tile_weighted_leverage_sketch_s8_kernel(
                 nc.tensor.transpose(htr[i][:, s * P : (s + 1) * P], words[:, s * P : (s + 1) * P], ident[:])
 
         def evac_ht(i, eng):
-            if i % 2 == 0:
+            if i // 2 not in htg_pair:
                 htg_pair[i // 2] = work.tile([P, 2, 1024], BF16, name="htg", tag="htg", align_bytes=64)
             htg[i] = htg_pair[i // 2][:, i % 2]
             evac_words(htg[i], htr[i], eng)
 
-        def quantize_ht(tiles):
-            for i in tiles:
-                assert i in htg
-            quantize_pair(tiles, hq_pair, hs_pair, htg_pair, hq, hs, "h")
+        def quantize_ht(pair):
+            for i in range(2):
+                assert 2 * pair + i in htg
+            q = work.tile([P, 512], U32, name="hq", tag="hq", align_bytes=64)
+            s = work.tile([P, 512], U8, name="hs", tag="hs", align_bytes=64)
+            nc.vector.quantize_mx(
+                out=q[:].bitcast(FP8X4), scales=s[:], in_=htg_pair[pair][:].rearrange("p i c -> p (i c)")
+            )
+            for i in range(2):
+                hq[2 * pair + i] = q[:, 256 * i : 256 * (i + 1)]
+                hs[2 * pair + i] = s[:, 256 * i : 256 * (i + 1)]
 
         yps = {}
 
@@ -262,7 +265,7 @@ def tile_weighted_leverage_sketch_s8_kernel(
         y_view = y.rearrange("(g p t) n -> g t p n", p=P, t=4)
 
         def evac_y(i, eng):
-            y_sb = work.tile([P, R], F32, name="y_sb", tag="y_sb", align_bytes=64)
+            y_sb = work.tile([P, R], F32, name="y_sb", tag="y_sb", bufs=5, align_bytes=64)
             if eng == "v":
                 nc.vector.tensor_copy(out=y_sb[:], in_=yps[i][:])
             else:
@@ -351,43 +354,49 @@ def tile_weighted_leverage_sketch_s8_kernel(
             pattern, head, tail = rule
             return "s" if i < head else "v" if i >= tail else pattern[i % len(pattern)]
 
-        for half in range(2):
+        for half in range(2 if MODE == 1 else 0):
             sps = bank("tr", PTR)
             for j in range(4):
                 c0 = 4 * half + j
                 nc.tensor.transpose(sps[:, j * P : (j + 1) * P], scale_v[:, c0 : c0 + 1].to_broadcast([P, P]), ident[:])
-            out = scale_sb[:].rearrange("p (k c) -> p k c", c=8)[:, :, 4 * half : 4 * half + 4]
-            in_ = sps[:].rearrange("p (c k) -> p k c", c=4)
-            if X_SC[half] == "v":
-                nc.vector.tensor_copy(out=out, in_=in_)
-            else:
-                nc.scalar.copy(out=out, in_=in_)
+            for i in range(2):
+                out = scale_sb[:, K * i : K * (i + 1)].rearrange("p (k c) -> p k c", c=8)[:, :, 4 * half : 4 * half + 4]
+                in_ = sps[:].rearrange("p (c k) -> p k c", c=4)
+                if X_SC[half] == "v":
+                    nc.vector.tensor_copy(out=out, in_=in_)
+                else:
+                    nc.scalar.copy(out=out, in_=in_)
         done = set()
-        mm_c_ready = []
+        qdone = set()
 
         def run(tok, pair):
-            i = 2 * pair + int(tok[-1])
-            h = int(tok[-2]) if tok[-2] in "01" else 0
-            k = tok[:2]
-            if k == "P0" or k == "P1":
-                if X_A2[i % len(X_A2)] == "1":
-                    product(i)
-            elif k == "W0" or k == "W1":
-                if X_A2[i % len(X_A2)] == "2":
-                    widen(i)
+            d = ""
+            for j, ch in enumerate(tok):
+                if ch in "01":
+                    k, d = tok[:j], tok[j:]
+                    break
+            else:
+                k = tok
+            i = 2 * pair + int(d[0]) if d else 0
+            if k == "P":
+                if MODE == 1:
+                    product(pair)
+            elif k == "MS":
+                if MODE == 2:
+                    claim(pair)
+            elif k == "W":
+                if MODE == 2:
+                    widen(pair, int(d))
             elif k == "TA":
-                transpose_a(i)
+                transpose_a(pair, int(d))
             elif k == "EA":
-                evac_a(i, eng(X_EA, i))
-            elif k == "QA" or k == "QH":
-                q = quantize_a if k == "QA" else quantize_ht
-                if pair in SINGLE:
-                    q([i])
-                elif i % 2 == 1:
-                    q([i - 1, i])
-            elif k == "HM":
-                mm_h(i, h)
-            elif k == "HE":
+                evac_a(pair, int(d))
+            elif k == "QA":
+                quantize_a(pair)
+            elif k == "M":
+                mm_h(i, int(d[1]))
+            elif k == "F":
+                h = int(d[1])
                 evac_h(i, h, eng(X_EE, 2 * i + h))
                 done.add((i, h))
             elif k == "TH":
@@ -395,51 +404,49 @@ def tile_weighted_leverage_sketch_s8_kernel(
                 transpose_h(i)
             elif k == "EH":
                 evac_ht(i, eng(X_EH, i))
-            elif k == "Y0" or k == "Y1":
+            elif k == "QH":
+                quantize_ht(pair)
+            elif k == "Y":
                 mm_y(i)
             elif k == "EY":
                 evac_y(i, eng(X_EY, i))
             elif k == "LV":
                 lev_y(i)
-            elif k == "IC" or k == "QC":
-                if pair % 2 == 1:
-                    h = int(tok[-1])
-                    for j in range(4):
-                        assert (2 * pair + 1 - j, h) in done
-                    (interleave_c if k == "IC" else quantize_c)(pair // 2, h)
-                    if k == "QC":
-                        qdone.add((pair // 2, h))
+            elif pair % 2 == 1:
+                h = int(d)
+                for j in range(4):
+                    assert (2 * pair + 1 - j, h) in done
+                (interleave_c if k == "IC" else quantize_c)(pair // 2, h)
+                if k == "QC":
+                    qdone.add((pair // 2, h))
 
-        qdone = set()
-        rinv_todo = list(RINV)
         cdone = 0
-        for s in range(-2, TILES // 2 + 8):
-            for tok, lag in ORDER:
+        bdone = set()
+        for s in range(-3, TILES // 2 + 9):
+            for tok, lag, per in ORDER:
                 if tok == "R":
-                    for x in [x for x in rinv_todo if x[0] == s + lag]:
+                    for x in [x for x in RINV if x[0] == s]:
                         if x[1] == "I":
                             interleave_rinv(x[2], x[3], x[4], x[5])
                         else:
                             quantize_rinv(x[2], x[3])
                 elif tok == "B":
-                    j = s - BSTART
-                    if 0 <= j < 3:
-                        transpose_b(j)
-                        evac_b(j, BENG)
+                    if 0 <= s - BSTART < 3:
+                        transpose_b(s - BSTART)
+                        evac_b(s - BSTART, BENG)
                 elif tok == "BQ":
-                    j = s - BSTART - lag
-                    if 0 <= j < 3:
-                        quantize_b(j)
-                elif tok == "C":
-                    while s >= CSTART and cdone < GROUPS and (cdone, 0) in qdone and (cdone, 1) in qdone:
-                        for h in range(2):
-                            mm_c(cdone, h)
-                        cdone += 1
+                    if 0 <= s - BSTART - lag < 3:
+                        quantize_b(s - BSTART - lag)
+                        bdone.add(s - BSTART - lag)
                 elif 0 <= s - lag < TILES // 2:
                     run(tok, s - lag)
+            while s >= CSTART and cdone < GROUPS and {(cdone, 0), (cdone, 1)} <= qdone and cdone // 2 in bdone:
+                for h in range(2):
+                    mm_c(cdone, h)
+                    if cdone == GROUPS - 1:
+                        evac_c(h, CENG[h])
+                cdone += 1
         assert cdone == GROUPS
-        for h in range(2):
-            evac_c(h, CENG[h])
 
         lps = bank("tr", PTR)
         for t in range(4):

@@ -20,17 +20,18 @@ SQUARE = mybir.ActivationFunctionType.Square
 
 P = 128
 X_DMA = ["a0", "r00", "r01", "a1", "r10", "r11", "a2", "j", "a3", "a4", "a5", "a6", "a7", "b", "a8", "a9", "a10", "a11"]
-X_SC = "ss"
+X_SC = "vs"
 X_A2 = ("1111", 0, 24)
 MODE = 2
+X_WV = 1
 PTR, PH, PY = 3, 3, 2
-ORDER = [("EY1", 6, 1), ("TA0", 0, 1), ("QH", 5, 1), ("P", -53, 1), ("TH0", 3, 1), ("F11", 2, 1), ("QA", 1, 1), ("EH1", 4, 1), ("IC1", 6, 1), ("LV1", 6, 1), ("B", 0, 1), ("IC0", 3, 1), ("R", 0, 1), ("MS", -1, 1), ("F00", 2, 1), ("EH0", 3, 1), ("Y0", 5, 1), ("QC0", 4, 1), ("BQ", 1, 1), ("TA1", 0, 1), ("M01", 1, 1), ("M10", 1, 1), ("EY0", 5, 1), ("EA0", 0, 1), ("LV0", 5, 1), ("EA1", 0, 1), ("Y1", 5, 1), ("F01", 1, 1), ("QC1", 8, 1), ("M11", 1, 1), ("M00", 1, 1), ("TH1", 3, 1), ("F10", 1, 1), ("W0", -1, 1), ("W1", -1, 1)]
-RINV = [(-3, "I", 0, 0, 1, "s"), (-2, "I", 0, 1, 1, "s"), (1, "I", 1, 1, 1, "v"), (1, "Q", 0, 0), (1, "Q", 0, 1), (-2, "I", 0, 0, 0, "s"), (1, "Q", 1, 0), (-2, "I", 1, 0, 1, "s"), (1, "Q", 1, 1), (-2, "I", 1, 0, 0, "s"), (0, "I", 0, 1, 0, "v"), (-2, "I", 1, 1, 0, "s")]
-X_EA = ("vvvv", 3, 21)
-X_EH = ("ssss", 12, 23)
-X_EY = ("ssss", 1, 24)
-X_EE = ("vsssssss", 12, 44)
-BSTART, BENG, CSTART, CENG = 13, "s", -58, "vv"
+ORDER = [("EH1", 3, 1), ("EA1", 0, 1), ("M11", 2, 1), ("Y1", 5, 1), ("EY0", 6, 1), ("LV0", 6, 1), ("W0", -1, 1), ("P", -4, 1), ("M00", 1, 1), ("F01", 2, 1), ("BQ", 1, 1), ("F11", 2, 1), ("QH", 4, 1), ("M10", 1, 1), ("EY1", 5, 1), ("IC1", 5, 1), ("QC0", 4, 1), ("B", 0, 1), ("QC1", 7, 1), ("W1", -1, 1), ("TH0", 2, 1), ("R", 0, 1), ("IC0", 2, 1), ("TH1", 2, 1), ("F00", 1, 1), ("LV1", 5, 1), ("MS", -2, 1), ("EH0", 2, 1), ("QA", 0, 1), ("TA0", -1, 1), ("EA0", -1, 1), ("Y0", 5, 1), ("TA1", -1, 1), ("F10", 1, 1), ("M01", 1, 1)]
+RINV = [(-2, "I", 0, 0, 0, "s"), (1, "I", 1, 0, 0, "s"), (1, "Q", 1, 1), (-2, "I", 0, 1, 0, "s"), (-2, "I", 0, 1, 1, "s"), (1, "Q", 1, 0), (0, "I", 1, 1, 1, "s"), (-2, "I", 1, 0, 1, "s"), (0, "I", 1, 1, 0, "s"), (0, "Q", 0, 1), (-1, "I", 0, 0, 1, "v"), (-1, "Q", 0, 0)]
+X_EA = ("vsss", 10, 23)
+X_EH = ("ssss", 10, 20)
+X_EY = ("ssss", 9, 24)
+X_EE = ("svssssss", 10, 46)
+BSTART, BENG, CSTART, CENG = 13, "s", -36, "vs"
 GROUPS = M // 512
 TILES = M // P
 KG = K // 512
@@ -51,7 +52,8 @@ def tile_weighted_leverage_sketch_s8_kernel(
             return psum.tile([P, 512], F32, name=kind, tag=kind, bufs=bufs)
 
         scale_v = keep.tile([P, 8], F32, name="scale_v", align_bytes=64)
-        nc.sync.dma_start(out=scale_v[:], in_=a_scale.rearrange("o (p c) -> p (o c)", p=P))
+        if MODE == 1:
+            nc.sync.dma_start(out=scale_v[:], in_=a_scale.rearrange("o (p c) -> p (o c)", p=P))
         scale_p = keep.tile([P, KG, 2, 2], F32, name="scale_p", align_bytes=64)
         nc.scalar.dma_start(out=scale_p[:].rearrange("p g u e -> p g (u e)"), in_=a_scale.rearrange("o (g p t) -> p (o g) t", p=P, t=4))
         scale_sb = keep.tile([P, 2 * K if MODE == 1 else 8], F32, name="scale_sb", align_bytes=64)
@@ -143,10 +145,17 @@ def tile_weighted_leverage_sketch_s8_kernel(
             )
 
         def claim(pair):
+            if pair < X_WV:
+                return
             ab[pair] = work.tile([P, 2, K], BF16, name="ab", tag="ab", align_bytes=64)
             nc.vector.memset(ab[pair][:, :, 0:2], 0.0)
 
         def widen(pair, i):
+            if pair < X_WV:
+                if i == 0:
+                    ab[pair] = work.tile([P, 2, K], BF16, name="ab", tag="ab", align_bytes=64)
+                nc.vector.tensor_copy(out=ab[pair][:, i, :], in_=a8[pair][:, i, :].bitcast(FP8))
+                return
             assert pair in ab
             nc.gpsimd.tensor_copy(out=ab[pair][:, i, :], in_=a8[pair][:, i, :].bitcast(FP8))
 
@@ -448,12 +457,13 @@ def tile_weighted_leverage_sketch_s8_kernel(
                 cdone += 1
         assert cdone == GROUPS
 
-        lps = bank("tr", PTR)
-        for t in range(4):
-            nc.tensor.transpose(lps[:, t * P : (t + 1) * P], lev_sb[:, t, :], ident[:])
         lev_rows = keep.tile([P, 512], F32, name="lev_rows", align_bytes=64)
-        nc.vector.tensor_copy(
-            out=lev_rows[:GROUPS, :].rearrange("g (p t) -> g p t", t=4),
-            in_=lps[:GROUPS, :].rearrange("g (t p) -> g p t", t=4),
-        )
+        for t0 in (0, 2):
+            lps = bank("tr", PTR)
+            for j in range(2):
+                nc.tensor.transpose(lps[:, j * P : (j + 1) * P], lev_sb[:, t0 + j, :], ident[:])
+            nc.vector.tensor_copy(
+                out=lev_rows[:GROUPS, :].rearrange("g (p t) -> g p t", t=4)[:, :, t0 : t0 + 2],
+                in_=lps[:GROUPS, : 2 * P].rearrange("g (t p) -> g p t", t=2),
+            )
         nc.sync.dma_start(out=lev.rearrange("(g m) -> g m", g=GROUPS), in_=lev_rows[:GROUPS, :])

from contextlib import ExitStack

import concourse.mybir as mybir
from concourse.masks import make_identity

M, K, N, R, T = 3072, 1024, 1024, 512, 128
FLOPS = 2 * M * K * N + 2 * M * N * R + 2 * T * M * N

F32 = mybir.dt.float32
BF16 = mybir.dt.bfloat16
I32 = mybir.dt.int32
U32 = mybir.dt.uint32
U8 = mybir.dt.uint8
FP8 = mybir.dt.float8_e4m3fn
FP8X4 = mybir.dt.float8_e4m3fn_x4
FP4X4 = mybir.dt.float4_e2m1fn_x4
MULT = mybir.AluOpType.mult
COPY = mybir.ActivationFunctionType.Copy
SQUARE = mybir.ActivationFunctionType.Square

P = 128
X_DMA = ["a0", "r00", "r01", "a1", "r10", "r11", "a2", "j", "a3", "a4", "a5", "a6", "a7", "b", "a8", "a9", "a10", "a11"]
X_SC = "vs"
X_A2 = ("1111", 0, 24)
MODE = 2
X_WV = 1
PTR, PH, PY = 3, 3, 2
ORDER = [("EH1", 3, 1), ("EA1", 0, 1), ("M11", 2, 1), ("Y1", 5, 1), ("EY0", 6, 1), ("LV0", 6, 1), ("W0", -1, 1), ("P", -4, 1), ("M00", 1, 1), ("F01", 2, 1), ("BQ", 1, 1), ("F11", 2, 1), ("QH", 4, 1), ("M10", 1, 1), ("EY1", 5, 1), ("IC1", 5, 1), ("QC0", 4, 1), ("B", 0, 1), ("QC1", 7, 1), ("W1", -1, 1), ("TH0", 2, 1), ("R", 0, 1), ("IC0", 2, 1), ("TH1", 2, 1), ("F00", 1, 1), ("LV1", 5, 1), ("MS", -2, 1), ("EH0", 2, 1), ("QA", 0, 1), ("TA0", -1, 1), ("EA0", -1, 1), ("Y0", 5, 1), ("TA1", -1, 1), ("F10", 1, 1), ("M01", 1, 1)]
RINV = [(-2, "I", 0, 0, 0, "s"), (1, "I", 1, 0, 0, "s"), (1, "Q", 1, 1), (-2, "I", 0, 1, 0, "s"), (-2, "I", 0, 1, 1, "s"), (1, "Q", 1, 0), (0, "I", 1, 1, 1, "s"), (-2, "I", 1, 0, 1, "s"), (0, "I", 1, 1, 0, "s"), (0, "Q", 0, 1), (-1, "I", 0, 0, 1, "v"), (-1, "Q", 0, 0)]
X_EA = ("vsss", 10, 23)
X_EH = ("ssss", 10, 20)
X_EY = ("ssss", 9, 24)
X_EE = ("svssssss", 10, 46)
BSTART, BENG, CSTART, CENG = 13, "s", -36, "vs"
GROUPS = M // 512
TILES = M // P
KG = K // 512
NG = N // 512


def tile_weighted_leverage_sketch_s8_kernel(
    tc, a_bytes, a_scale, rinv, w, jl_words, jl_scales, b, y, lev, c
):
    nc = tc.nc
    with ExitStack() as ctx:
        keep = ctx.enter_context(tc.tile_pool(name="keep", bufs=1))
        work = ctx.enter_context(tc.tile_pool(name="work", bufs=3))
        psum = ctx.enter_context(tc.psum_pool(name="psum", bufs=1))
        ctx.enter_context(tc.manual_schedule())

        def bank(kind, bufs):
            return psum.tile([P, 512], F32, name=kind, tag=kind, bufs=bufs)

        scale_v = keep.tile([P, 8], F32, name="scale_v", align_bytes=64)
        if MODE == 1:
            nc.sync.dma_start(out=scale_v[:], in_=a_scale.rearrange("o (p c) -> p (o c)", p=P))
        scale_p = keep.tile([P, KG, 2, 2], F32, name="scale_p", align_bytes=64)
        nc.scalar.dma_start(out=scale_p[:].rearrange("p g u e -> p g (u e)"), in_=a_scale.rearrange("o (g p t) -> p (o g) t", p=P, t=4))
        scale_sb = keep.tile([P, 2 * K if MODE == 1 else 8], F32, name="scale_sb", align_bytes=64)
        w_bf = keep.tile([P, GROUPS, 4], BF16, name="w_bf", align_bytes=64)
        nc.scalar.dma_start(out=w_bf[:], in_=w.rearrange("(g p t) -> p g t", p=P, t=4))

        ident = keep.tile([P, P], F32, name="ident", align_bytes=64)
        make_identity(nc, ident[:])
        jsc = keep.tile([P, NG, R], U8, name="jsc", align_bytes=64)
        nc.gpsimd.memset(jsc[:].rearrange("p g n -> p (g n)").bitcast(I32), 0)
        lev_sb = keep.tile([P, 4, P], F32, name="lev_sb", align_bytes=64)
        nc.gpsimd.memset(lev_sb[:], 0.0)

        warm = keep.tile([P, 1], F32, name="warm")
        nc.scalar.activation(out=warm[:], in_=ident[:, 0:1], func=SQUARE)

        a_view = a_bytes.rearrange("(g p t) k -> g p t k", p=P, t=4)
        a8 = {}

        def load_a(pair):
            g, t0 = pair // 2, 2 * (pair % 2)
            a8[pair] = keep.tile([P, 2, K], U8, name=f"a8_{pair}", align_bytes=64)
            nc.sync.dma_start(out=a8[pair][:], in_=a_view[g, :, t0 : t0 + 2, :])

        raw = {}

        def load_rinv(h, g):
            raw[h, g] = keep.tile([P, 4, 512], BF16, name=f"raw_{h}{g}", align_bytes=64)
            nc.sync.dma_start(
                out=raw[h, g][:],
                in_=rinv.rearrange("(g p t) n -> g p t n", p=P, t=4)[g, :, :, 512 * h : 512 * (h + 1)],
            )

        jw = keep.tile([P, NG, 2 * R], U8, name="jw", align_bytes=64)
        jsc_i = jsc[:].rearrange("p g n -> p (g n)").bitcast(I32)
        b_sb = keep.tile([P, M], BF16, name="b_sb", align_bytes=64)
        for item in X_DMA:
            if item[0] == "a":
                load_a(int(item[1:]))
            elif item[0] == "r":
                load_rinv(int(item[1]), int(item[2]))
            elif item[0] == "b":
                nc.sync.dma_start(out=b_sb[:], in_=b)
            else:
                nc.sync.dma_start(out=jw[:], in_=jl_words.rearrange("g p n -> p g n"))
                for q in range(4):
                    nc.sync.dma_start(
                        out=jsc_i[32 * q : 32 * q + 4, :].rearrange("p (g n) -> p g n", g=NG),
                        in_=jl_scales[:, 4 * q : 4 * q + 4, :].bitcast(I32).rearrange("g q n -> q g n"),
                    )

        w_sb = keep.tile([P, GROUPS * 4], F32, name="w_sb", align_bytes=64)
        nc.gpsimd.tensor_copy(out=w_sb[:], in_=w_bf[:].rearrange("p g t -> p (g t)"))

        rq = keep.tile([P, KG, N], U32, name="rq", align_bytes=64)
        rs = keep.tile([P, KG, N], U8, name="rs", align_bytes=64)
        rg = {}

        def interleave_rinv(h, g, u, eng):
            if (h, g) not in rg:
                rg[h, g] = keep.tile([P, 512, 4], BF16, name=f"rg_{h}{g}", align_bytes=64)
            dst = rg[h, g][:].rearrange("p (u q e) t -> p u q t e", u=2, e=2)[:, u]
            src = raw[h, g][:].rearrange("p t (q u e) -> p u q t e", u=2, e=2)[:, u]
            if eng == "v":
                nc.vector.tensor_copy(out=dst, in_=src)
            else:
                nc.scalar.copy(out=dst, in_=src)
            rdone.add((h, g, u))

        rdone = set()

        def quantize_rinv(h, g):
            assert (h, g, 0) in rdone and (h, g, 1) in rdone
            cols = slice(512 * h, 512 * (h + 1))
            nc.vector.quantize_mx(
                out=rq[:, g, cols].bitcast(FP8X4), scales=rs[:, g, cols], in_=rg[h, g][:].rearrange("p n t -> p (n t)")
            )

        ag_pair, aq_pair, as_pair, htg_pair, hq_pair, hs_pair = {}, {}, {}, {}, {}, {}
        ab, atr, ag, aq, asc = {}, {}, {}, {}, {}

        def product(pair):
            ab[pair] = work.tile([P, 2, K], BF16, name="ab", tag="ab", align_bytes=64)
            nc.vector.tensor_tensor(
                out=ab[pair][:].rearrange("p i k -> p (i k)"),
                in0=a8[pair][:].rearrange("p i k -> p (i k)").bitcast(FP8),
                in1=scale_sb[:],
                op=MULT,
            )

        def claim(pair):
            if pair < X_WV:
                return
            ab[pair] = work.tile([P, 2, K], BF16, name="ab", tag="ab", align_bytes=64)
            nc.vector.memset(ab[pair][:, :, 0:2], 0.0)

        def widen(pair, i):
            if pair < X_WV:
                if i == 0:
                    ab[pair] = work.tile([P, 2, K], BF16, name="ab", tag="ab", align_bytes=64)
                nc.vector.tensor_copy(out=ab[pair][:, i, :], in_=a8[pair][:, i, :].bitcast(FP8))
                return
            assert pair in ab
            nc.gpsimd.tensor_copy(out=ab[pair][:, i, :], in_=a8[pair][:, i, :].bitcast(FP8))

        def transpose_a(pair, g):
            atr[pair, g] = bank("tr", PTR)
            for u in range(2):
                for i in range(2):
                    s = 2 * u + i
                    words = ab[pair][:, i, :].bitcast(F32)
                    nc.tensor.transpose(
                        atr[pair, g][:, s * P : (s + 1) * P], words[:, 256 * g + u : 256 * (g + 1) : 2], ident[:]
                    )

        def evac_words(dst, src, eng):
            out = dst.bitcast(F32).rearrange("p (g r u) -> p g r u", g=2, u=2)
            in_ = src[:].rearrange("p (g u r) -> p g r u", g=2, u=2)
            if eng == "v":
                nc.vector.tensor_copy(out=out, in_=in_)
            else:
                nc.scalar.copy(out=out, in_=in_)

        def evac_a(pair, g):
            if pair not in ag:
                ag[pair] = work.tile([P, KG, 1024], BF16, name="ag", tag="ag", align_bytes=64)
            if MODE == 2:
                nc.vector.tensor_tensor(
                    out=ag[pair][:, g].rearrange("p (c u e) -> p c u e", u=2, e=2),
                    in0=atr[pair, g][:].bitcast(BF16).rearrange("p (u c e) -> p c u e", u=2, e=2),
                    in1=scale_p[:, g].unsqueeze(1).to_broadcast([P, 2 * P, 2, 2]),
                    op=MULT,
                )
            else:
                out = ag[pair][:, g].bitcast(F32).rearrange("p (c u) -> p c u", u=2)
                in_ = atr[pair, g][:].rearrange("p (u c) -> p c u", u=2)
                if eng(X_EA, 2 * pair + g) == "v":
                    nc.vector.tensor_copy(out=out, in_=in_)
                else:
                    nc.scalar.copy(out=out, in_=in_)

        def quantize_a(pair):
            q = work.tile([P, 512], U32, name="aq", tag="aq", align_bytes=64)
            s = work.tile([P, 512], U8, name="asc", tag="asc", align_bytes=64)
            nc.vector.quantize_mx(out=q[:].bitcast(FP8X4), scales=s[:], in_=ag[pair][:].rearrange("p g c -> p (g c)"))
            for i in range(2):
                aq[2 * pair + i] = q[:].rearrange("p (g i m) -> p i g m", g=KG, i=2)[:, i]
                asc[2 * pair + i] = s[:].rearrange("p (g i m) -> p i g m", g=KG, i=2)[:, i]

        hps, hb = {}, {}

        def mm_h(i, h):
            hps[i, h] = bank("h", PH)
            for g in range(KG):
                cols = slice(512 * h, 512 * (h + 1))
                nc.tensor.matmul_mx(
                    out=hps[i, h][:],
                    lhsT=aq[i][:, g].bitcast(FP8X4),
                    lhsT_scale=asc[i][:, g],
                    rhs=rq[:, g, cols].bitcast(FP8X4),
                    rhs_scale=rs[:, g, cols],
                    start=(g == 0),
                    stop=(g == KG - 1),
                )

        def evac_h(i, h, eng):
            gg, t = i // 4, i % 4
            if gg not in hb:
                hb[gg] = work.tile([P, 4, N], BF16, name="hb", tag="hb", align_bytes=64)
            dst = hb[gg][:, t, 512 * h : 512 * (h + 1)]
            if eng == "v":
                nc.vector.tensor_scalar(out=dst, in0=hps[i, h][:], scalar1=w_sb[:, i : i + 1], scalar2=None, op0=MULT)
            else:
                nc.scalar.activation(out=dst, in_=hps[i, h][:], func=COPY, scale=w_sb[:, i : i + 1])

        htr, htg, hq, hs = {}, {}, {}, {}

        def transpose_h(i):
            htr[i] = bank("tr", PTR)
            words = hb[i // 4][:, i % 4, :].bitcast(F32)
            for s in range(4):
                nc.tensor.transpose(htr[i][:, s * P : (s + 1) * P], words[:, s * P : (s + 1) * P], ident[:])

        def evac_ht(i, eng):
            if i // 2 not in htg_pair:
                htg_pair[i // 2] = work.tile([P, 2, 1024], BF16, name="htg", tag="htg", align_bytes=64)
            htg[i] = htg_pair[i // 2][:, i % 2]
            evac_words(htg[i], htr[i], eng)

        def quantize_ht(pair):
            for i in range(2):
                assert 2 * pair + i in htg
            q = work.tile([P, 512], U32, name="hq", tag="hq", align_bytes=64)
            s = work.tile([P, 512], U8, name="hs", tag="hs", align_bytes=64)
            nc.vector.quantize_mx(
                out=q[:].bitcast(FP8X4), scales=s[:], in_=htg_pair[pair][:].rearrange("p i c -> p (i c)")
            )
            for i in range(2):
                hq[2 * pair + i] = q[:, 256 * i : 256 * (i + 1)]
                hs[2 * pair + i] = s[:, 256 * i : 256 * (i + 1)]

        yps = {}

        def mm_y(i):
            yps[i] = bank("y", PY)
            for g in range(NG):
                rows = slice(g * P, (g + 1) * P)
                nc.tensor.matmul_mx(
                    out=yps[i][:],
                    lhsT=hq[i][:, rows].bitcast(FP8X4),
                    lhsT_scale=hs[i][:, rows],
                    rhs=jw[:, g, :].bitcast(FP4X4),
                    rhs_scale=jsc[:, g, :],
                    start=(g == 0),
                    stop=(g == NG - 1),
                )

        y_view = y.rearrange("(g p t) n -> g t p n", p=P, t=4)

        def evac_y(i, eng):
            y_sb = work.tile([P, R], F32, name="y_sb", tag="y_sb", bufs=5, align_bytes=64)
            if eng == "v":
                nc.vector.tensor_copy(out=y_sb[:], in_=yps[i][:])
            else:
                nc.scalar.copy(out=y_sb[:], in_=yps[i][:])
            nc.sync.dma_start(out=y_view[i // 4, i % 4], in_=y_sb[:])

        def lev_y(i):
            sq = work.tile([P, R], BF16, name="sq", tag="sq", align_bytes=64)
            nc.scalar.activation(
                out=sq[:], in_=yps[i][:], func=SQUARE, scale=R**-0.5,
                accum_out=lev_sb[:, i % 4, i // 4 : i // 4 + 1],
            )

        cg, cq, cs = {}, {}, {}

        def interleave_c(gg, h):
            cg[gg, h] = work.tile([P, 512, 4], BF16, name="cg", tag="cg", align_bytes=64)
            nc.vector.tensor_copy(
                out=cg[gg, h][:].rearrange("p (c i) t -> p c t i", i=4),
                in_=hb[gg][:, :, 512 * h : 512 * (h + 1)].rearrange("p t (c i) -> p c t i", i=4),
            )

        def quantize_c(gg, h):
            cq[gg, h] = keep.tile([P, 512], U32, name=f"cq_{gg}{h}", align_bytes=64)
            cs[gg, h] = keep.tile([P, 512], U8, name=f"cs_{gg}{h}", align_bytes=64)
            nc.vector.quantize_mx(
                out=cq[gg, h][:].bitcast(FP8X4), scales=cs[gg, h][:], in_=cg[gg, h][:].rearrange("p n t -> p (n t)")
            )

        btr = {}
        bg = keep.tile([P, 6, P, 4], BF16, name="bg", align_bytes=64)
        bq = keep.tile([P, 6 * P], U32, name="bq", align_bytes=64)
        bs = keep.tile([P, 6 * P], U8, name="bs", align_bytes=64)

        def transpose_b(j):
            btr[j] = bank("tr", PTR)
            words = b_sb[:].bitcast(F32)
            for s in range(4):
                g, u = 2 * j + s // 2, s % 2
                nc.tensor.transpose(btr[j][:, s * P : (s + 1) * P], words[:, 256 * g + u : 256 * (g + 1) : 2], ident[:])

        def evac_b(j, eng):
            out = bg[:, 2 * j : 2 * j + 2].rearrange("p g r t -> p (g r t)").bitcast(F32).rearrange(
                "p (g r u) -> p g r u", g=2, u=2
            )
            in_ = btr[j][:].rearrange("p (g u r) -> p g r u", g=2, u=2)
            if eng == "v":
                nc.vector.tensor_copy(out=out, in_=in_)
            else:
                nc.scalar.copy(out=out, in_=in_)

        def quantize_b(j):
            cols = slice(256 * j, 256 * (j + 1))
            nc.vector.quantize_mx(
                out=bq[:, cols].bitcast(FP8X4), scales=bs[:, cols],
                in_=bg[:, 2 * j : 2 * j + 2].rearrange("p g r t -> p (g r t)"),
            )

        cps = {}

        def mm_c(gg, h):
            if gg == 0:
                cps[h] = bank("h", PH)
            rows = slice(gg * P, (gg + 1) * P)
            nc.tensor.matmul_mx(
                out=cps[h][:],
                lhsT=bq[:, rows].bitcast(FP8X4),
                lhsT_scale=bs[:, rows],
                rhs=cq[gg, h][:].bitcast(FP8X4),
                rhs_scale=cs[gg, h][:],
                start=(gg == 0),
                stop=(gg == GROUPS - 1),
            )

        def evac_c(h, eng):
            c_sb = work.tile([P, 512], F32, name="c_sb", tag="c_sb", align_bytes=64)
            out = c_sb[:].rearrange("p (q u e) -> p q u e", u=2, e=2)
            in_ = cps[h][:].rearrange("p (u q e) -> p q u e", u=2, e=2)
            if eng == "v":
                nc.vector.tensor_copy(out=out, in_=in_)
            else:
                nc.scalar.copy(out=out, in_=in_)
            nc.sync.dma_start(out=c[:, 512 * h : 512 * (h + 1)], in_=c_sb[:])

        def eng(rule, i):
            pattern, head, tail = rule
            return "s" if i < head else "v" if i >= tail else pattern[i % len(pattern)]

        for half in range(2 if MODE == 1 else 0):
            sps = bank("tr", PTR)
            for j in range(4):
                c0 = 4 * half + j
                nc.tensor.transpose(sps[:, j * P : (j + 1) * P], scale_v[:, c0 : c0 + 1].to_broadcast([P, P]), ident[:])
            for i in range(2):
                out = scale_sb[:, K * i : K * (i + 1)].rearrange("p (k c) -> p k c", c=8)[:, :, 4 * half : 4 * half + 4]
                in_ = sps[:].rearrange("p (c k) -> p k c", c=4)
                if X_SC[half] == "v":
                    nc.vector.tensor_copy(out=out, in_=in_)
                else:
                    nc.scalar.copy(out=out, in_=in_)
        done = set()
        qdone = set()

        def run(tok, pair):
            d = ""
            for j, ch in enumerate(tok):
                if ch in "01":
                    k, d = tok[:j], tok[j:]
                    break
            else:
                k = tok
            i = 2 * pair + int(d[0]) if d else 0
            if k == "P":
                if MODE == 1:
                    product(pair)
            elif k == "MS":
                if MODE == 2:
                    claim(pair)
            elif k == "W":
                if MODE == 2:
                    widen(pair, int(d))
            elif k == "TA":
                transpose_a(pair, int(d))
            elif k == "EA":
                evac_a(pair, int(d))
            elif k == "QA":
                quantize_a(pair)
            elif k == "M":
                mm_h(i, int(d[1]))
            elif k == "F":
                h = int(d[1])
                evac_h(i, h, eng(X_EE, 2 * i + h))
                done.add((i, h))
            elif k == "TH":
                assert (i, 0) in done and (i, 1) in done
                transpose_h(i)
            elif k == "EH":
                evac_ht(i, eng(X_EH, i))
            elif k == "QH":
                quantize_ht(pair)
            elif k == "Y":
                mm_y(i)
            elif k == "EY":
                evac_y(i, eng(X_EY, i))
            elif k == "LV":
                lev_y(i)
            elif pair % 2 == 1:
                h = int(d)
                for j in range(4):
                    assert (2 * pair + 1 - j, h) in done
                (interleave_c if k == "IC" else quantize_c)(pair // 2, h)
                if k == "QC":
                    qdone.add((pair // 2, h))

        cdone = 0
        bdone = set()
        for s in range(-3, TILES // 2 + 9):
            for tok, lag, per in ORDER:
                if tok == "R":
                    for x in [x for x in RINV if x[0] == s]:
                        if x[1] == "I":
                            interleave_rinv(x[2], x[3], x[4], x[5])
                        else:
                            quantize_rinv(x[2], x[3])
                elif tok == "B":
                    if 0 <= s - BSTART < 3:
                        transpose_b(s - BSTART)
                        evac_b(s - BSTART, BENG)
                elif tok == "BQ":
                    if 0 <= s - BSTART - lag < 3:
                        quantize_b(s - BSTART - lag)
                        bdone.add(s - BSTART - lag)
                elif 0 <= s - lag < TILES // 2:
                    run(tok, s - lag)
            while s >= CSTART and cdone < GROUPS and {(cdone, 0), (cdone, 1)} <= qdone and cdone // 2 in bdone:
                for h in range(2):
                    mm_c(cdone, h)
                    if cdone == GROUPS - 1:
                        evac_c(h, CENG[h])
                cdone += 1
        assert cdone == GROUPS

        lev_rows = keep.tile([P, 512], F32, name="lev_rows", align_bytes=64)
        for t0 in (0, 2):
            lps = bank("tr", PTR)
            for j in range(2):
                nc.tensor.transpose(lps[:, j * P : (j + 1) * P], lev_sb[:, t0 + j, :], ident[:])
            nc.vector.tensor_copy(
                out=lev_rows[:GROUPS, :].rearrange("g (p t) -> g p t", t=4)[:, :, t0 : t0 + 2],
                in_=lps[:GROUPS, : 2 * P].rearrange("g (t p) -> g p t", t=2),
            )
        nc.sync.dma_start(out=lev.rearrange("(g m) -> g m", g=GROUPS), in_=lev_rows[:GROUPS, :])
